import numpy as np
import ml_dtypes


def mxq(x, axis, fmt="e4m3"):
    dtype, down = {"e4m3": (ml_dtypes.float8_e4m3fn, 7), "e5m2": (ml_dtypes.float8_e5m2, 14)}[fmt]
    v = np.moveaxis(np.asarray(x, np.float32).astype(ml_dtypes.bfloat16).astype(np.float64), axis, -1)
    blocks = v.reshape(v.shape[:-1] + (-1, 32))
    amax = np.abs(blocks).max(-1, keepdims=True)
    byte = np.maximum(np.where(amax > 0, np.frexp(amax)[1] - 1 + 127, 0) - down, 1)
    scale = np.exp2(byte - 127.0)
    codes = (blocks / scale).astype(np.float32).astype(dtype).astype(np.float64)
    return np.moveaxis((codes * scale).reshape(v.shape), -1, axis)


WIDE = False


def mx_kscale(k):
    if not WIDE:
        return np.ones(k)
    levels = np.array([10, -10, 5, -5, 0])
    if k % 512:
        return np.exp2(np.random.permutation(np.resize(levels, k // 32))).repeat(32)
    a = np.empty((k // 512, 16))
    for p in range(k // 512):
        a[p, :8] = np.random.permutation(np.resize(levels, 8))
        for g in range(8):
            far = levels[np.abs(levels - a[p, g]) >= 10]
            a[p, g + 8] = far[np.random.randint(len(far))]
    return np.exp2(a.ravel()).repeat(32)


def f64(x):
    return np.asarray(x).astype(np.float64)


def striped(idx):
    return np.tile(idx.reshape(-1, 16).T, (8, 1)).astype(np.uint16)


def unstriped(offs):
    return offs[:16].T.reshape(-1).astype(np.int64)


def pack_weight(w):
    k, n = w.shape
    w = f64(np.asarray(w, np.float32).astype(ml_dtypes.bfloat16)).reshape(k // 32, 32, n)
    amax = np.abs(w).max(1)
    byte = np.clip(np.where(amax > 0, np.frexp(amax)[1] - 1 + 127 - 7, 1), 1, 254)
    scaled = (w * np.exp2(127.0 - byte)[:, None, :]).reshape(k, n).astype(np.float32)
    words = np.ascontiguousarray(scaled.reshape(k // 512, 128, 4, n).transpose(0, 1, 3, 2)).astype(ml_dtypes.float8_e4m3fn).view(np.uint8)
    return words, np.ascontiguousarray(byte.astype(np.uint8).reshape(k // 512, 16, n))


def unpack_weight(words, scales):
    g, p, n, _ = words.shape
    vals = np.ascontiguousarray(words).view(ml_dtypes.float8_e4m3fn).astype(np.float64) * np.repeat(np.exp2(scales.astype(np.float64) - 127.0), 8, axis=1)[..., None]
    return vals.transpose(0, 1, 3, 2).reshape(g * 512, n)


K, T, E, C, N = 1024, 512, 2, 256, 512


def by_expert(wq, xq):
    return np.concatenate([wq[e].T @ xq[:, e * C:(e + 1) * C] for e in range(E)], axis=1)


def setup_inputs():
    n = np.random.standard_normal
    s = mx_kscale(K)[:, None]
    packed = [pack_weight(m) for m in n((E, K, N)) / np.sqrt(K) / s[None]]
    return {
        "xT": (n((K, T)) * s).astype(np.float32),
        "w_words": np.stack([m[0] for m in packed]),
        "w_scales": np.stack([m[1] for m in packed]),
        "gate": np.tile(np.random.uniform(0.2, 1.0, E * C), (N, 1)).astype(np.float32),
        "offs": striped(np.random.permutation(T)[:E * C]),
    }


def reference(xT, w_words, w_scales, gate, offs):
    idx = unstriped(offs)
    xq = mxq(f64(xT)[:, idx], 0, "e4m3")
    w = np.stack([unpack_weight(w_words[e], w_scales[e]) for e in range(E)])
    y = by_expert(w, xq)
    out = np.zeros((N, T))
    out[:, idx] = f64(gate) * y
    return out

@@ -1,0 +1,174 @@
+from contextlib import ExitStack
+
+import concourse.mybir as mybir
+
+K, T, E, C, N = 1024, 512, 2, 256, 512
+FLOPS = 2 * K * N * E * C
+
+F32 = mybir.dt.float32
+BF16 = mybir.dt.bfloat16
+U32 = mybir.dt.uint32
+I32 = mybir.dt.int32
+U16 = mybir.dt.uint16
+U8 = mybir.dt.uint8
+FP8X4 = mybir.dt.float8_e4m3fn_x4
+MULT = mybir.AluOpType.mult
+COPY = mybir.ActivationFunctionType.Copy
+
+P = 128
+PASSES = K // 512
+BLOCKS = N // P
+LIST_COLS = C // 16
+
+
+def tile_routed_moe_kernel(tc, xT, w_words, w_scales, gate, offs, out):
+    nc = tc.nc
+    with ExitStack() as ctx:
+        lists = ctx.enter_context(tc.tile_pool(name="lists", bufs=1))
+        keep = ctx.enter_context(tc.tile_pool(name="keep", bufs=1))
+        psum = ctx.enter_context(tc.psum_pool(name="psum", bufs=1))
+
+        offsets = lists.tile([P, E * C // 16], U16, name="offsets")
+        nc.sync.dma_start(offsets[:], offs)
+
+        def slots(e):
+            return offsets[:, e * LIST_COLS : (e + 1) * LIST_COLS]
+
+        warm = keep.tile([P, 2], F32, name="warm")
+        nc.vector.memset(warm[:, 0:1], 0.0)
+        nc.scalar.copy(warm[:, 1:2], warm[:, 0:1])
+
+        w_planes = keep.tile([P, N], U8, name="w_planes", align_bytes=64)
+        nc.vector.memset(w_planes[:].bitcast(I32), 0)
+
+        x_rows = xT.rearrange("(g p t) n -> g p t n", p=P, t=4)
+        raw = {}
+        for u in range(2):
+            for g in range(PASSES):
+                raw[g, u] = keep.tile([P, 2, T], F32, name="raw%d%d" % (g, u))
+                nc.sync.dma_start(raw[g, u][:], x_rows[g, :, 2 * u : 2 * u + 2, :])
+
+        s_rows = w_scales.rearrange("e a q n -> (e a) q n")
+        for q in range(4):
+            nc.sync.dma_start(
+                w_planes[32 * q : 32 * q + 16, :].bitcast(I32),
+                s_rows[:, 4 * q : 4 * q + 4, :].bitcast(I32),
+            )
+        w_codes = keep.tile([P, E * PASSES, N], U32, name="w_codes", align_bytes=64)
+        gates = keep.tile([P, BLOCKS, E * C], F32, name="gates")
+        nc.sync.dma_start(
+            w_codes[:, 0:PASSES, :].bitcast(I32),
+            w_words[0].rearrange("a p n r -> p a (n r)").bitcast(I32),
+        )
+        nc.sync.dma_start(gates[:], gate.rearrange("(b p) j -> p b j", p=P))
+        nc.sync.dma_start(
+            w_codes[:, PASSES : 2 * PASSES, :].bitcast(I32),
+            w_words[1].rearrange("a p n r -> p a (n r)").bitcast(I32),
+        )
+
+        grouped = {}
+        x_codes = {}
+        x_planes = {}
+
+        def new_grouped(g, e, tag):
+            grouped[g, e] = keep.tile([P, C, 4], BF16, name="grouped%d%d" % (g, e), tag=tag, align_bytes=64)
+
+        planes = {}
+
+        def plane_cast(u):
+            planes[u] = keep.tile([P, 2, T], BF16, name="planes%d" % u, tag="planes%d" % u, align_bytes=64)
+            nc.vector.tensor_copy(out=planes[u][:], in_=raw[0, u][:])
+
+        def scalar_gather(e, u):
+            for h in range(2):
+                nc.scalar.activation(grouped[0, e][:, :, 2 * u + h], planes[u][:, h, :].indirect(slots(e)), COPY)
+
+        pair = {}
+
+        def pair_cast(u):
+            pair[u] = keep.tile([P, T, 2], BF16, name="pair%d" % u, align_bytes=64)
+            nc.vector.tensor_copy(out=pair[u][:], in_=raw[1, u][:].rearrange("p h n -> p n h"))
+
+        def vector_gather(e, u):
+            words = grouped[1, e][:].rearrange("p c t -> p (c t)").bitcast(U32)
+            nc.vector.tensor_copy(
+                words.rearrange("p (c u) -> p c u", u=2)[:, :, u],
+                pair[u][:].rearrange("p n h -> p (n h)").bitcast(U32).indirect(slots(e)),
+            )
+
+        def quantize(g, e, tag):
+            x_codes[g, e] = keep.tile([P, C], U32, name="x_codes%d%d" % (g, e), tag=tag, align_bytes=64)
+            x_planes[g, e] = keep.tile([P, C], U8, name="x_planes%d%d" % (g, e), align_bytes=64)
+            nc.vector.quantize_mx(
+                out=x_codes[g, e][:].bitcast(FP8X4),
+                scales=x_planes[g, e][:],
+                in_=grouped[g, e][:].rearrange("p c t -> p (c t)"),
+            )
+
+        acc = {}
+        for e in range(E):
+            for b in range(BLOCKS):
+                acc[e, b] = psum.tile([P, C], F32, name="acc%d%d" % (e, b))
+
+        def multiply(e, g, first):
+            j = e * PASSES + g
+            for b in range(BLOCKS):
+                cols = slice(b * P, (b + 1) * P)
+                nc.tensor.matmul_mx(
+                    out=acc[e, b][:],
+                    lhsT=w_codes[:, j, cols].bitcast(FP8X4),
+                    lhsT_scale=w_planes[4 * j : P, cols],
+                    rhs=x_codes[g, e][:].bitcast(FP8X4),
+                    rhs_scale=x_planes[g, e][:],
+                    start=first,
+                    stop=not first,
+                )
+
+        windows = {}
+        for b in range(BLOCKS):
+            windows[b] = keep.tile([P, T], F32, name="window%d" % b)
+        sums = {}
+
+        def empty(e, b):
+            sums[e, b] = keep.tile([P, C], F32, name="sums%d%d" % (e, b), tag=("planes1" if (e, b) == (0, 3) else "sums%d%d" % (e, b)), align_bytes=64)
+            nc.scalar.copy(sums[e, b][:], acc[e, b][:])
+
+        def scatter(e, b):
+            nc.vector.tensor_tensor(windows[b][:].indirect(slots(e)), sums[e, b][:], gates[:, b, e * C : (e + 1) * C], MULT)
+            if e == E - 1:
+                nc.sync.dma_start(out[b * P : (b + 1) * P, :], windows[b][:])
+
+        new_grouped(0, 0, "slot_b")
+        new_grouped(1, 0, "slot_a")
+        plane_cast(0)
+        scalar_gather(0, 0)
+        pair_cast(0)
+        vector_gather(0, 0)
+        plane_cast(1)
+        scalar_gather(0, 1)
+        pair_cast(1)
+        vector_gather(0, 1)
+        quantize(1, 0, "codes10")
+        multiply(0, 1, True)
+        quantize(0, 0, "slot_a")
+        multiply(0, 0, False)
+        new_grouped(1, 1, "slot_b")
+        vector_gather(1, 0)
+        vector_gather(1, 1)
+        quantize(1, 1, "codes11")
+        multiply(1, 1, True)
+        for b in range(BLOCKS - 1):
+            empty(0, b)
+        new_grouped(0, 1, "slot_a")
+        scalar_gather(1, 0)
+        scalar_gather(1, 1)
+        empty(0, 3)
+        scatter(0, 0)
+        scatter(0, 1)
+        scatter(0, 2)
+        quantize(0, 1, "codes01")
+        multiply(1, 0, False)
+        scatter(0, 3)
+        for b in range(BLOCKS):
+            empty(1, b)
+            scatter(1, b)

@@ -13,6 +13,7 @@ U16 = mybir.dt.uint16
 U8 = mybir.dt.uint8
 FP8X4 = mybir.dt.float8_e4m3fn_x4
 MULT = mybir.AluOpType.mult
+ADD = mybir.AluOpType.add
 COPY = mybir.ActivationFunctionType.Copy
 
 P = 128
@@ -77,7 +78,10 @@ def tile_routed_moe_kernel(tc, xT, w_words, w_scales, gate, offs, out):
 
         def plane_cast(u):
             planes[u] = keep.tile([P, 2, T], BF16, name="planes%d" % u, tag="planes%d" % u, align_bytes=64)
-            nc.vector.tensor_copy(out=planes[u][:], in_=raw[0, u][:])
+            if u == 0:
+                nc.vector.tensor_copy(out=planes[u][:], in_=raw[0, u][:])
+            else:
+                nc.gpsimd.tensor_scalar(planes[u][:], raw[0, u][:], 1.0, 0.0, MULT, ADD)
 
         def scalar_gather(e, u):
             for h in range(2):
@@ -95,6 +99,17 @@ def tile_routed_moe_kernel(tc, xT, w_words, w_scales, gate, offs, out):
                 words.rearrange("p (c u) -> p c u", u=2)[:, :, u],
                 pair[u][:].rearrange("p n h -> p (n h)").bitcast(U32).indirect(slots(e)),
             )
+
+        early = keep.tile([P, C, 2], BF16, name="early", align_bytes=64)
+
+        def early_gather():
+            nc.vector.tensor_copy(
+                early[:].rearrange("p c h -> p (c h)").bitcast(U32),
+                pair[0][:].rearrange("p n h -> p (n h)").bitcast(U32).indirect(slots(1)),
+            )
+
+        def place_early():
+            nc.scalar.copy(grouped[1, 1][:, :, 0:2], early[:])
 
         def quantize(g, e, tag):
             x_codes[g, e] = keep.tile([P, C], U32, name="x_codes%d%d" % (g, e), tag=tag, align_bytes=64)
@@ -144,6 +159,7 @@ def tile_routed_moe_kernel(tc, xT, w_words, w_scales, gate, offs, out):
         scalar_gather(0, 0)
         pair_cast(0)
         vector_gather(0, 0)
+        early_gather()
         plane_cast(1)
         scalar_gather(0, 1)
         pair_cast(1)
@@ -153,7 +169,7 @@ def tile_routed_moe_kernel(tc, xT, w_words, w_scales, gate, offs, out):
         quantize(0, 0, "slot_a")
         multiply(0, 0, False)
         new_grouped(1, 1, "slot_b")
-        vector_gather(1, 0)
+        place_early()
         vector_gather(1, 1)
         quantize(1, 1, "codes11")
         multiply(1, 1, True)

@@ -125,19 +125,22 @@ def tile_routed_moe_kernel(tc, xT, w_words, w_scales, gate, offs, out):
             for b in range(BLOCKS):
                 acc[e, b] = psum.tile([P, C], F32, name="acc%d%d" % (e, b))
 
-        def multiply(e, g, first):
+        def multiply_block(e, g, b, opens):
             j = e * PASSES + g
+            cols = slice(b * P, (b + 1) * P)
+            nc.tensor.matmul_mx(
+                out=acc[e, b][:],
+                lhsT=w_codes[:, j, cols].bitcast(FP8X4),
+                lhsT_scale=w_planes[4 * j : P, cols],
+                rhs=x_codes[g, e][:].bitcast(FP8X4),
+                rhs_scale=x_planes[g, e][:],
+                start=opens,
+                stop=not opens,
+            )
+
+        def multiply(e, g, opens):
             for b in range(BLOCKS):
-                cols = slice(b * P, (b + 1) * P)
-                nc.tensor.matmul_mx(
-                    out=acc[e, b][:],
-                    lhsT=w_codes[:, j, cols].bitcast(FP8X4),
-                    lhsT_scale=w_planes[4 * j : P, cols],
-                    rhs=x_codes[g, e][:].bitcast(FP8X4),
-                    rhs_scale=x_planes[g, e][:],
-                    start=first,
-                    stop=not first,
-                )
+                multiply_block(e, g, b, opens)
 
         windows = {}
         for b in range(BLOCKS):
@@ -164,10 +167,13 @@ def tile_routed_moe_kernel(tc, xT, w_words, w_scales, gate, offs, out):
         scalar_gather(0, 1)
         pair_cast(1)
         vector_gather(0, 1)
-        quantize(1, 0, "codes10")
-        multiply(0, 1, True)
+        quantize(1, 0, "slot_c")
+        multiply_block(0, 1, 0, True)
         quantize(0, 0, "slot_a")
-        multiply(0, 0, False)
+        multiply_block(0, 0, 0, False)
+        for b in range(1, BLOCKS):
+            multiply_block(0, 0, b, True)
+            multiply_block(0, 1, b, False)
         new_grouped(1, 1, "slot_b")
         place_early()
         vector_gather(1, 1)
@@ -175,7 +181,7 @@ def tile_routed_moe_kernel(tc, xT, w_words, w_scales, gate, offs, out):
         multiply(1, 1, True)
         for b in range(BLOCKS - 1):
             empty(0, b)
-        new_grouped(0, 1, "slot_a")
+        new_grouped(0, 1, "slot_c")
         scalar_gather(1, 0)
         scalar_gather(1, 1)
         empty(0, 3)

@@ -30,7 +30,6 @@ def tile_routed_moe_kernel(tc, xT, w_words, w_scales, gate, offs, out):
         psum = ctx.enter_context(tc.psum_pool(name="psum", bufs=1))
 
         offsets = lists.tile([P, E * C // 16], U16, name="offsets")
-        nc.sync.dma_start(offsets[:], offs)
 
         def slots(e):
             return offsets[:, e * LIST_COLS : (e + 1) * LIST_COLS]
@@ -48,6 +47,8 @@ def tile_routed_moe_kernel(tc, xT, w_words, w_scales, gate, offs, out):
             for g in range(PASSES):
                 raw[g, u] = keep.tile([P, 2, T], F32, name="raw%d%d" % (g, u))
                 nc.sync.dma_start(raw[g, u][:], x_rows[g, :, 2 * u : 2 * u + 2, :])
+                if (g, u) == (0, 0):
+                    nc.sync.dma_start(offsets[:], offs)
 
         s_rows = w_scales.rearrange("e a q n -> (e a) q n")
         for q in range(4):
@@ -100,16 +101,13 @@ def tile_routed_moe_kernel(tc, xT, w_words, w_scales, gate, offs, out):
                 pair[u][:].rearrange("p n h -> p (n h)").bitcast(U32).indirect(slots(e)),
             )
 
-        early = keep.tile([P, C, 2], BF16, name="early", align_bytes=64)
+        def late_planes():
+            planes[2] = keep.tile([P, 2, T], BF16, name="planes2", align_bytes=64)
+            nc.gpsimd.tensor_scalar(planes[2][:], raw[1, 1][:], 1.0, 0.0, MULT, ADD)
 
-        def early_gather():
-            nc.vector.tensor_copy(
-                early[:].rearrange("p c h -> p (c h)").bitcast(U32),
-                pair[0][:].rearrange("p n h -> p (n h)").bitcast(U32).indirect(slots(1)),
-            )
-
-        def place_early():
-            nc.scalar.copy(grouped[1, 1][:, :, 0:2], early[:])
+        def late_gather():
+            for h in range(2):
+                nc.scalar.activation(grouped[1, 1][:, :, 2 + h], planes[2][:, h, :].indirect(slots(1)), COPY)
 
         def quantize(g, e, tag):
             x_codes[g, e] = keep.tile([P, C], U32, name="x_codes%d%d" % (g, e), tag=tag, align_bytes=64)
@@ -162,10 +160,12 @@ def tile_routed_moe_kernel(tc, xT, w_words, w_scales, gate, offs, out):
         scalar_gather(0, 0)
         pair_cast(0)
         vector_gather(0, 0)
-        early_gather()
+        new_grouped(1, 1, "slot_d")
+        vector_gather(1, 0)
         plane_cast(1)
         scalar_gather(0, 1)
         pair_cast(1)
+        late_planes()
         vector_gather(0, 1)
         quantize(1, 0, "slot_c")
         multiply_block(0, 1, 0, True)
@@ -174,9 +174,7 @@ def tile_routed_moe_kernel(tc, xT, w_words, w_scales, gate, offs, out):
         for b in range(1, BLOCKS):
             multiply_block(0, 0, b, True)
             multiply_block(0, 1, b, False)
-        new_grouped(1, 1, "slot_b")
-        place_early()
-        vector_gather(1, 1)
+        late_gather()
         quantize(1, 1, "codes11")
         multiply(1, 1, True)
         for b in range(BLOCKS - 1):

from contextlib import ExitStack

import concourse.mybir as mybir

K, T, E, C, N = 1024, 512, 2, 256, 512
FLOPS = 2 * K * N * E * C

F32 = mybir.dt.float32
BF16 = mybir.dt.bfloat16
U32 = mybir.dt.uint32
I32 = mybir.dt.int32
U16 = mybir.dt.uint16
U8 = mybir.dt.uint8
FP8X4 = mybir.dt.float8_e4m3fn_x4
MULT = mybir.AluOpType.mult
ADD = mybir.AluOpType.add
COPY = mybir.ActivationFunctionType.Copy

P = 128
PASSES = K // 512
BLOCKS = N // P
LIST_COLS = C // 16


def tile_routed_moe_kernel(tc, xT, w_words, w_scales, gate, offs, out):
    nc = tc.nc
    with ExitStack() as ctx:
        lists = ctx.enter_context(tc.tile_pool(name="lists", bufs=1))
        keep = ctx.enter_context(tc.tile_pool(name="keep", bufs=1))
        psum = ctx.enter_context(tc.psum_pool(name="psum", bufs=1))

        offsets = lists.tile([P, E * C // 16], U16, name="offsets")

        def slots(e):
            return offsets[:, e * LIST_COLS : (e + 1) * LIST_COLS]

        warm = keep.tile([P, 2], F32, name="warm")
        nc.vector.memset(warm[:, 0:1], 0.0)
        nc.scalar.copy(warm[:, 1:2], warm[:, 0:1])

        w_planes = keep.tile([P, N], U8, name="w_planes", align_bytes=64)
        nc.vector.memset(w_planes[:].bitcast(I32), 0)

        x_rows = xT.rearrange("(g p t) n -> g p t n", p=P, t=4)
        raw = {}
        for u in range(2):
            for g in range(PASSES):
                raw[g, u] = keep.tile([P, 2, T], F32, name="raw%d%d" % (g, u))
                nc.sync.dma_start(raw[g, u][:], x_rows[g, :, 2 * u : 2 * u + 2, :])
                if (g, u) == (0, 0):
                    nc.sync.dma_start(offsets[:], offs)

        s_rows = w_scales.rearrange("e a q n -> (e a) q n")
        for q in range(4):
            nc.sync.dma_start(
                w_planes[32 * q : 32 * q + 16, :].bitcast(I32),
                s_rows[:, 4 * q : 4 * q + 4, :].bitcast(I32),
            )
        w_codes = keep.tile([P, E * PASSES, N], U32, name="w_codes", align_bytes=64)
        gates = keep.tile([P, BLOCKS, E * C], F32, name="gates")
        nc.sync.dma_start(
            w_codes[:, 0:PASSES, :].bitcast(I32),
            w_words[0].rearrange("a p n r -> p a (n r)").bitcast(I32),
        )
        nc.sync.dma_start(gates[:], gate.rearrange("(b p) j -> p b j", p=P))
        nc.sync.dma_start(
            w_codes[:, PASSES : 2 * PASSES, :].bitcast(I32),
            w_words[1].rearrange("a p n r -> p a (n r)").bitcast(I32),
        )

        grouped = {}
        x_codes = {}
        x_planes = {}

        def new_grouped(g, e, tag):
            grouped[g, e] = keep.tile([P, C, 4], BF16, name="grouped%d%d" % (g, e), tag=tag, align_bytes=64)

        planes = {}

        def plane_cast(u):
            planes[u] = keep.tile([P, 2, T], BF16, name="planes%d" % u, tag="planes%d" % u, align_bytes=64)
            if u == 0:
                nc.vector.tensor_copy(out=planes[u][:], in_=raw[0, u][:])
            else:
                nc.gpsimd.tensor_scalar(planes[u][:], raw[0, u][:], 1.0, 0.0, MULT, ADD)

        def scalar_gather(e, u):
            for h in range(2):
                nc.scalar.activation(grouped[0, e][:, :, 2 * u + h], planes[u][:, h, :].indirect(slots(e)), COPY)

        pair = {}

        def pair_cast(u):
            pair[u] = keep.tile([P, T, 2], BF16, name="pair%d" % u, align_bytes=64)
            nc.vector.tensor_copy(out=pair[u][:], in_=raw[1, u][:].rearrange("p h n -> p n h"))

        def vector_gather(e, u):
            words = grouped[1, e][:].rearrange("p c t -> p (c t)").bitcast(U32)
            nc.vector.tensor_copy(
                words.rearrange("p (c u) -> p c u", u=2)[:, :, u],
                pair[u][:].rearrange("p n h -> p (n h)").bitcast(U32).indirect(slots(e)),
            )

        def late_planes():
            planes[2] = keep.tile([P, 2, T], BF16, name="planes2", align_bytes=64)
            nc.gpsimd.tensor_scalar(planes[2][:], raw[1, 1][:], 1.0, 0.0, MULT, ADD)

        def late_gather():
            for h in range(2):
                nc.scalar.activation(grouped[1, 1][:, :, 2 + h], planes[2][:, h, :].indirect(slots(1)), COPY)

        def quantize(g, e, tag):
            x_codes[g, e] = keep.tile([P, C], U32, name="x_codes%d%d" % (g, e), tag=tag, align_bytes=64)
            x_planes[g, e] = keep.tile([P, C], U8, name="x_planes%d%d" % (g, e), align_bytes=64)
            nc.vector.quantize_mx(
                out=x_codes[g, e][:].bitcast(FP8X4),
                scales=x_planes[g, e][:],
                in_=grouped[g, e][:].rearrange("p c t -> p (c t)"),
            )

        acc = {}
        for e in range(E):
            for b in range(BLOCKS):
                acc[e, b] = psum.tile([P, C], F32, name="acc%d%d" % (e, b))

        def multiply_block(e, g, b, opens):
            j = e * PASSES + g
            cols = slice(b * P, (b + 1) * P)
            nc.tensor.matmul_mx(
                out=acc[e, b][:],
                lhsT=w_codes[:, j, cols].bitcast(FP8X4),
                lhsT_scale=w_planes[4 * j : P, cols],
                rhs=x_codes[g, e][:].bitcast(FP8X4),
                rhs_scale=x_planes[g, e][:],
                start=opens,
                stop=not opens,
            )

        def multiply(e, g, opens):
            for b in range(BLOCKS):
                multiply_block(e, g, b, opens)

        windows = {}
        for b in range(BLOCKS):
            windows[b] = keep.tile([P, T], F32, name="window%d" % b)
        sums = {}

        def empty(e, b):
            sums[e, b] = keep.tile([P, C], F32, name="sums%d%d" % (e, b), tag=("planes1" if (e, b) == (0, 3) else "sums%d%d" % (e, b)), align_bytes=64)
            nc.scalar.copy(sums[e, b][:], acc[e, b][:])

        def scatter(e, b):
            nc.vector.tensor_tensor(windows[b][:].indirect(slots(e)), sums[e, b][:], gates[:, b, e * C : (e + 1) * C], MULT)
            if e == E - 1:
                nc.sync.dma_start(out[b * P : (b + 1) * P, :], windows[b][:])

        new_grouped(0, 0, "slot_b")
        new_grouped(1, 0, "slot_a")
        plane_cast(0)
        scalar_gather(0, 0)
        pair_cast(0)
        vector_gather(0, 0)
        new_grouped(1, 1, "slot_d")
        vector_gather(1, 0)
        plane_cast(1)
        scalar_gather(0, 1)
        pair_cast(1)
        late_planes()
        vector_gather(0, 1)
        quantize(1, 0, "slot_c")
        multiply_block(0, 1, 0, True)
        quantize(0, 0, "slot_a")
        multiply_block(0, 0, 0, False)
        for b in range(1, BLOCKS):
            multiply_block(0, 0, b, True)
            multiply_block(0, 1, b, False)
        late_gather()
        quantize(1, 1, "codes11")
        multiply(1, 1, True)
        for b in range(BLOCKS - 1):
            empty(0, b)
        new_grouped(0, 1, "slot_c")
        scalar_gather(1, 0)
        scalar_gather(1, 1)
        empty(0, 3)
        scatter(0, 0)
        scatter(0, 1)
        scatter(0, 2)
        quantize(0, 1, "codes01")
        multiply(1, 0, False)
        scatter(0, 3)
        for b in range(BLOCKS):
            empty(1, b)
            scatter(1, b)
